import numpy as np
import ml_dtypes


def mxq(x, axis, fmt="e4m3"):
    dtype, down = {"e4m3": (ml_dtypes.float8_e4m3fn, 7), "e5m2": (ml_dtypes.float8_e5m2, 14)}[fmt]
    v = np.moveaxis(np.asarray(x, np.float32).astype(ml_dtypes.bfloat16).astype(np.float64), axis, -1)
    blocks = v.reshape(v.shape[:-1] + (-1, 32))
    amax = np.abs(blocks).max(-1, keepdims=True)
    byte = np.maximum(np.where(amax > 0, np.frexp(amax)[1] - 1 + 127, 0) - down, 1)
    scale = np.exp2(byte - 127.0)
    codes = (blocks / scale).astype(np.float32).astype(dtype).astype(np.float64)
    return np.moveaxis((codes * scale).reshape(v.shape), -1, axis)


WIDE = False


def mx_kscale(k):
    if not WIDE:
        return np.ones(k)
    levels = np.array([10, -10, 5, -5, 0])
    if k % 512:
        return np.exp2(np.random.permutation(np.resize(levels, k // 32))).repeat(32)
    a = np.empty((k // 512, 16))
    for p in range(k // 512):
        a[p, :8] = np.random.permutation(np.resize(levels, 8))
        for g in range(8):
            far = levels[np.abs(levels - a[p, g]) >= 10]
            a[p, g + 8] = far[np.random.randint(len(far))]
    return np.exp2(a.ravel()).repeat(32)


def f64(x):
    return np.asarray(x).astype(np.float64)


def striped(idx):
    return np.tile(idx.reshape(-1, 16).T, (8, 1)).astype(np.uint16)


def unstriped(offs):
    return offs[:16].T.reshape(-1).astype(np.int64)


def pack_weight(w):
    k, n = w.shape
    w = f64(np.asarray(w, np.float32).astype(ml_dtypes.bfloat16)).reshape(k // 32, 32, n)
    amax = np.abs(w).max(1)
    byte = np.clip(np.where(amax > 0, np.frexp(amax)[1] - 1 + 127 - 7, 1), 1, 254)
    scaled = (w * np.exp2(127.0 - byte)[:, None, :]).reshape(k, n).astype(np.float32)
    words = np.ascontiguousarray(scaled.reshape(k // 512, 128, 4, n).transpose(0, 1, 3, 2)).astype(ml_dtypes.float8_e4m3fn).view(np.uint8)
    return words, np.ascontiguousarray(byte.astype(np.uint8).reshape(k // 512, 16, n))


def unpack_weight(words, scales):
    g, p, n, _ = words.shape
    vals = np.ascontiguousarray(words).view(ml_dtypes.float8_e4m3fn).astype(np.float64) * np.repeat(np.exp2(scales.astype(np.float64) - 127.0), 8, axis=1)[..., None]
    return vals.transpose(0, 1, 3, 2).reshape(g * 512, n)


E2M1 = np.array([0.0, 0.5, 1.0, 1.5, 2.0, 3.0, 4.0, 6.0, -0.0, -0.5, -1.0, -1.5, -2.0, -3.0, -4.0, -6.0])


def pack_fp4(w):
    k, n = w.shape
    w = f64(np.asarray(w, np.float32).astype(ml_dtypes.bfloat16)).reshape(k // 32, 32, n)
    amax = np.abs(w).max(1)
    mant, ex = np.frexp(amax / 6.0)
    byte = np.clip(np.where(amax > 0, np.where(mant > 0.5, ex, ex - 1) + 127, 1), 1, 254)
    scaled = (w * np.exp2(127.0 - byte)[:, None, :]).reshape(k, n).astype(np.float32)
    c = np.ascontiguousarray(scaled.reshape(k // 512, 128, 4, n).transpose(0, 1, 3, 2)).astype(ml_dtypes.float4_e2m1fn).view(np.uint8) & 0xF
    words = (c[..., 0::2] | (c[..., 1::2] << 4)).reshape(k // 512, 128, 2 * n)
    return np.ascontiguousarray(words), np.ascontiguousarray(byte.astype(np.uint8).reshape(k // 512, 16, n))


def unpack_fp4(words, scales):
    g, _, n = scales.shape
    words = np.ascontiguousarray(words).reshape(g, 128, n, 2)
    nib = np.empty((g, 128, n, 4), np.uint8)
    nib[..., 0::2] = words & 0xF
    nib[..., 1::2] = words >> 4
    vals = E2M1[nib] * np.repeat(np.exp2(scales.astype(np.float64) - 127.0), 8, axis=1)[..., None]
    return vals.transpose(0, 1, 3, 2).reshape(g * 512, n)


def planes(y):
    n, m = y.shape
    v = y.astype(np.float32).astype(ml_dtypes.bfloat16).astype(np.float64).reshape(n // 32, 32, m)
    top = np.abs(v).max(1)
    byte = np.clip(np.where(top > 0, np.frexp(top)[1] - 1 + 127 - 7, 1), 1, 254)
    codes = (v * np.exp2(127.0 - byte)[:, None, :]).reshape(n, m).astype(np.float32).astype(ml_dtypes.float8_e4m3fn).view(np.uint8)
    words = codes.reshape(n // 512, 128, 4, m).transpose(0, 1, 3, 2)
    return np.ascontiguousarray(words), np.ascontiguousarray(byte.astype(np.uint8).reshape(n // 512, 16, m))


K, T, S, N, H = 512, 1024, 512, 512, 512


def setup_inputs():
    n = np.random.standard_normal
    s = mx_kscale(K)[:, None]
    u = mx_kscale(H)
    packed_xT = pack_weight(n((K, T)) * s)
    packed_w1 = pack_fp4(n((K, N)) / np.sqrt(K) / s)
    packed_w2 = pack_fp4(n((H, N)) / np.sqrt(H) / u[:, None])
    return {
        "x_words": packed_xT[0],
        "x_scales": packed_xT[1],
        "w1_words": packed_w1[0],
        "w1_scales": packed_w1[1],
        "ef": (0.6 * n((H, S))).astype(np.float32),
        "unit": (np.random.uniform(0.6, 1.4, (H, 1)) * u[:, None]).astype(np.float32),
        "w2_words": packed_w2[0],
        "w2_scales": packed_w2[1],
        "offs": striped(np.random.permutation(T)[:S]),
        "r1": striped(np.random.permutation(S)),
        "r2": striped(np.random.permutation(S)),
        "r3": striped(np.random.permutation(S)),
    }


def reference(x_words, x_scales, w1_words, w1_scales, ef, unit, w2_words, w2_scales, offs, r1, r2, r3):
    xq = unpack_weight(x_words, x_scales)[:, unstriped(offs)]
    y = unpack_fp4(w1_words, w1_scales).T @ xq
    a1 = y[:, unstriped(r1)]
    st1 = y + a1
    a2 = st1[:, unstriped(r2)]
    st2 = st1 + a2
    efk = f64(ef) + np.tanh(st2)
    a3 = efk[:, unstriped(r3)]
    st3 = st2 - (1.5 * a3)
    b3 = st1[:, unstriped(r3)]
    hid = f64(unit) * np.maximum(st3, b3)
    out_0 = unpack_fp4(w2_words, w2_scales).T @ mxq(hid, 0, "e4m3")
    return (out_0,) + planes(out_0)

@@ -1,0 +1,214 @@
+from contextlib import ExitStack
+
+import concourse.mybir as mybir
+
+K, T, S, N, H = 512, 1024, 512, 512, 512
+FLOPS = 2 * K * H * S + 2 * H * N * S
+
+F32 = mybir.dt.float32
+BF16 = mybir.dt.bfloat16
+I32 = mybir.dt.int32
+U32 = mybir.dt.uint32
+U16 = mybir.dt.uint16
+U8 = mybir.dt.uint8
+FP8X4 = mybir.dt.float8_e4m3fn_x4
+FP4X4 = mybir.dt.float4_e2m1fn_x4
+ALU = mybir.AluOpType
+ACT = mybir.ActivationFunctionType
+
+P = 128
+PACK = 4
+SPARE = 16
+NOUT = 128
+G1 = "VSVS"
+G2 = "WSWS"
+G3 = "VVSS"
+O2 = "SSSV"
+PIECES = [128,128,128,128]
+ORDER = "A0 A1 A2 A3 B0 B1 B2 B3 C0 C1"
+WHOLE = [int(s[1]) for s in ORDER.split() if s[0] == "C"]
+
+
+def tile_picked_yrecdbl_max_po_kernel(
+    tc, x_words, x_scales, w1_words, w1_scales, ef, unit, w2_words, w2_scales, offs, r1, r2, r3, out_0, out_1, out_2
+):
+    nc = tc.nc
+    with ExitStack() as ctx:
+        sb = ctx.enter_context(tc.tile_pool(name="sb", bufs=1))
+        ps = ctx.enter_context(tc.psum_pool(name="ps", bufs=1))
+
+        def tile(name, shape, dtype):
+            return sb.tile(shape, dtype, name=name, align_bytes=64)
+
+        def load_list(name, src):
+            t = tile(name, [P, S // 16], U16)
+            nc.sync.dma_start(t[:], src)
+            return t
+
+        def load_scales(name, src, width, queue):
+            t = tile(name, [P, width], U8)
+            for g in range(4):
+                rows = src[0, 4 * g : 4 * g + 4, :].bitcast(I32)
+                queue.dma_start(t[32 * g : 32 * g + 32, :].bitcast(I32), rows.unsqueeze(0).to_broadcast([8, 4, width // 4]))
+            return t
+
+        def load_bytes(name, src, queue):
+            t = tile(name, [P, 2 * N], U8)
+            queue.dma_start(t[:].bitcast(I32), src[0].bitcast(I32))
+            return t
+
+        def deal(name, words, scales):
+            dw = tile(name + "_dw", [P, 2 * N], U8)
+            ds = tile(name + "_ds", [P, N], U8)
+            nc.vector.tensor_copy(
+                out=dw[:].rearrange("p (t m b) -> p t m b", t=PACK, b=2),
+                in_=words[:].rearrange("p (m t b) -> p t m b", t=PACK, b=2),
+            )
+            nc.vector.tensor_copy(
+                out=ds[:].rearrange("p (t m) -> p t m", t=PACK),
+                in_=scales[:].rearrange("p (m t) -> p t m", t=PACK),
+            )
+            return dw, ds
+
+        offs_t = load_list("offs_t", offs)
+        xs = load_scales("xs", x_scales, T, nc.scalar)
+        w1w = load_bytes("w1w", w1_words, nc.sync)
+        xw = tile("xw", [P, T], I32)
+        nc.sync.dma_start(xw[:], x_words[0].rearrange("p n t -> p (n t)").bitcast(I32))
+        w1s = load_scales("w1s", w1_scales, N, nc.scalar)
+        r1_t = load_list("r1_t", r1)
+        w2w = load_bytes("w2w", w2_words, nc.sync)
+        w2s = load_scales("w2s", w2_scales, N, nc.sync)
+        r2_t = load_list("r2_t", r2)
+        r3_t = load_list("r3_t", r3)
+        unit_t = tile("unit_t", [P, PACK], F32)
+        nc.sync.dma_start(unit_t[:], unit.rearrange("(p t) o -> p (t o)", t=PACK))
+        ef_t = tile("ef_t", [P, PACK, S], F32)
+        nc.sync.dma_start(ef_t[:], ef.rearrange("(p t) j -> p t j", t=PACK))
+
+        y = [tile(f"y{t}", [P, S + SPARE], F32) for t in range(PACK)]
+        st1 = [tile(f"st1_{t}", [P, S + SPARE], F32) for t in range(PACK)]
+        efk = [tile(f"efk{t}", [P, S + SPARE], F32) for t in range(PACK)]
+        for w in y + st1 + efk:
+            nc.gpsimd.memset(w[:, S:], 0.0)
+
+        xs_g = tile("xs_g", [P, S], U8)
+        xw_g = tile("xw_g", [P, S], U32)
+        nc.vector.tensor_copy(xs_g[:], xs[:].indirect(offs_t[:]))
+        w1d, w1sd = deal("w1", w1w, w1s)
+        nc.vector.tensor_copy(xw_g[:], xw[:].bitcast(U32).indirect(offs_t[:]))
+
+        ybank = [ps.tile([P, S], F32, name=f"ybank{t}") for t in range(PACK)]
+        for t in range(PACK):
+            nc.tensor.matmul_mx(
+                out=ybank[t][:],
+                lhsT=w1d[:, 2 * P * t : 2 * P * (t + 1)].bitcast(FP4X4),
+                lhsT_scale=w1sd[:, P * t : P * (t + 1)],
+                rhs=xw_g[:].bitcast(FP8X4),
+                rhs_scale=xs_g[:],
+                start=True,
+                stop=True,
+            )
+        w2d, w2sd = deal("w2", w2w, w2s)
+        gain = tile("gain", [P, PACK], F32)
+        nc.vector.tensor_scalar(gain[:], unit_t[:], -1.5, None, ALU.mult)
+
+        def add_partner(name, how, out, window, offsets):
+            other = tile(name, [P, S], F32)
+            if how == "S":
+                nc.scalar.activation(other[:], window[:].indirect(offsets[:]), ACT.Copy)
+                nc.vector.tensor_tensor(out, other[:], window[:, :S], ALU.add)
+                return
+            if how == "V":
+                nc.vector.tensor_copy(other[:], window[:, :S])
+            elif how == "W":
+                nc.scalar.copy(other[:], window[:, :S])
+            else:
+                nc.sync.dma_start(other[:], window[:, :S])
+            nc.vector.tensor_tensor(out, window[:].indirect(offsets[:]), other[:], ALU.add)
+
+        st2 = [tile(f"st2_{t}", [P, S], F32) for t in range(PACK)]
+        low = tile("low", [P, PACK, S], F32)
+
+        def round1(t):
+            nc.scalar.activation(y[t][:, :S], ybank[t][:], ACT.Copy, scale=-1.0 / 1.5)
+            add_partner(f"a1_{t}", G1[t], st1[t][:, :S], y[t], r1_t)
+
+        def round2(t):
+            add_partner(f"a2_{t}", G2[t], st2[t][:], st1[t], r2_t)
+            th = tile(f"th{t}", [P, S], F32)
+            nc.scalar.activation(th[:], st2[t][:], ACT.Tanh, scale=-1.5)
+            nc.vector.tensor_tensor(efk[t][:, :S], th[:], ef_t[:, t, :], ALU.add)
+
+        def round3(t, c0, n):
+            cols = slice(c0, c0 + n)
+            sel = r3_t[:, c0 // 16 : (c0 + n) // 16]
+            b3 = tile(f"b3_{t}_{c0}", [P, n], F32)
+            st3 = tile(f"st3_{t}_{c0}", [P, n], F32)
+            nc.scalar.activation(b3[:], st1[t][:].indirect(sel), ACT.Copy)
+            if G3[t] == "V":
+                nc.vector.tensor_tensor(st3[:], efk[t][:].indirect(sel), st2[t][:, cols], ALU.add)
+            else:
+                a3 = tile(f"a3_{t}_{c0}", [P, n], F32)
+                nc.scalar.activation(a3[:], efk[t][:].indirect(sel), ACT.Copy)
+                nc.vector.tensor_tensor(st3[:], a3[:], st2[t][:, cols], ALU.add)
+            nc.vector.tensor_tensor(low[:, t, cols], st3[:], b3[:], ALU.min)
+
+        for step in ORDER.split():
+            t = int(step[1])
+            if step[0] == "A":
+                round1(t)
+            elif step[0] == "B":
+                round2(t)
+            else:
+                round3(t, 0, S)
+
+        out_rows = out_0.rearrange("(p t) j -> p t j", t=PACK)
+        out_words = out_1[0].rearrange("p n t -> p (n t)").bitcast(I32)
+        o_scales = tile("o_scales", [P, S], U8)
+        c0 = 0
+        for i, n in enumerate(PIECES):
+            for t in range(PACK):
+                if t not in WHOLE:
+                    round3(t, c0, n)
+            hid = tile(f"hid{i}", [P, n * PACK], BF16)
+            nc.vector.tensor_tensor(
+                hid[:].rearrange("p (c i t) -> p c t i", i=2, t=PACK),
+                low[:, :, c0 : c0 + n].rearrange("p t (c i) -> p c t i", i=2),
+                gain[:].unsqueeze(1).unsqueeze(3).to_broadcast([P, n // 2, PACK, 2]),
+                ALU.mult,
+            )
+            h_codes = tile(f"h_codes{i}", [P, n], U32)
+            h_scales = tile(f"h_scales{i}", [P, n], U8)
+            nc.vector.quantize_mx(out=h_codes[:].bitcast(FP8X4), scales=h_scales[:], in_=hid[:])
+            for k0 in range(0, n, NOUT):
+                q = (c0 + k0) // NOUT
+                ocols = slice(c0 + k0, c0 + k0 + NOUT)
+                bank = ps.tile([P, PACK, NOUT], F32, name=f"obank{q}")
+                for t in range(PACK):
+                    nc.tensor.matmul_mx(
+                        out=bank[:, t, :],
+                        lhsT=w2d[:, 2 * P * t : 2 * P * (t + 1)].bitcast(FP4X4),
+                        lhsT_scale=w2sd[:, P * t : P * (t + 1)],
+                        rhs=h_codes[:, k0 : k0 + NOUT].bitcast(FP8X4),
+                        rhs_scale=h_scales[:, k0 : k0 + NOUT],
+                        start=True,
+                        stop=True,
+                    )
+                ob = tile(f"ob{q}", [P, NOUT * PACK], BF16)
+                ob_view = ob[:].rearrange("p (c i t) -> p c t i", i=2, t=PACK)
+                bank_view = bank[:].rearrange("p t (c i) -> p c t i", i=2)
+                if O2[q] == "S":
+                    nc.scalar.copy(ob_view, bank_view)
+                else:
+                    nc.vector.tensor_copy(ob_view, bank_view)
+                of = tile(f"of{q}", [P, PACK, NOUT], F32)
+                nc.scalar.copy(of[:], bank[:])
+                nc.sync.dma_start(out_rows[:, :, ocols], of[:])
+                o_codes = tile(f"o_codes{q}", [P, NOUT], I32)
+                nc.vector.quantize_mx(out=o_codes[:].bitcast(FP8X4), scales=o_scales[:, ocols], in_=ob[:])
+                nc.sync.dma_start(out_words[:, ocols], o_codes[:])
+            c0 = c0 + n
+        for g in range(4):
+            queue = nc.sync if g % 2 == 0 else nc.scalar
+            queue.dma_start(out_2[0, 4 * g : 4 * g + 4, :].bitcast(I32), o_scales[32 * g : 32 * g + 4, :].bitcast(I32))

@@ -20,12 +20,16 @@ P = 128
 PACK = 4
 SPARE = 16
 NOUT = 128
-G1 = "VSVS"
-G2 = "WSWS"
-G3 = "VVSS"
-O2 = "SSSV"
+G1 = "VVSS"
+G2 = "WWSS"
+G3 = "VVVS"
+O2 = "SSVV"
 PIECES = [128,128,128,128]
-ORDER = "A0 A1 A2 A3 B0 B1 B2 B3 C0 C1"
+EV = "SSSS"
+UM = "SSSS"
+IL = "VVVV"
+G4 = "SSSS"
+ORDER = "A0 A1 A2 A3 B0 B1 B2 B3 C0 C1 C2 D3"
 WHOLE = [int(s[1]) for s in ORDER.split() if s[0] == "C"]
 
 
@@ -57,25 +61,28 @@ def tile_picked_yrecdbl_max_po_kernel(
             queue.dma_start(t[:].bitcast(I32), src[0].bitcast(I32))
             return t
 
-        def deal(name, words, scales):
+        def deal_words(name, words):
             dw = tile(name + "_dw", [P, 2 * N], U8)
-            ds = tile(name + "_ds", [P, N], U8)
             nc.vector.tensor_copy(
                 out=dw[:].rearrange("p (t m b) -> p t m b", t=PACK, b=2),
                 in_=words[:].rearrange("p (m t b) -> p t m b", t=PACK, b=2),
             )
+            return dw
+
+        def deal_scales(name, scales):
+            ds = tile(name + "_ds", [P, N], U8)
             nc.vector.tensor_copy(
                 out=ds[:].rearrange("p (t m) -> p t m", t=PACK),
                 in_=scales[:].rearrange("p (m t) -> p t m", t=PACK),
             )
-            return dw, ds
+            return ds
 
         offs_t = load_list("offs_t", offs)
-        xs = load_scales("xs", x_scales, T, nc.scalar)
         w1w = load_bytes("w1w", w1_words, nc.sync)
+        xs = load_scales("xs", x_scales, T, nc.sync)
         xw = tile("xw", [P, T], I32)
         nc.sync.dma_start(xw[:], x_words[0].rearrange("p n t -> p (n t)").bitcast(I32))
-        w1s = load_scales("w1s", w1_scales, N, nc.scalar)
+        w1s = load_scales("w1s", w1_scales, N, nc.sync)
         r1_t = load_list("r1_t", r1)
         w2w = load_bytes("w2w", w2_words, nc.sync)
         w2s = load_scales("w2s", w2_scales, N, nc.sync)
@@ -92,24 +99,28 @@ def tile_picked_yrecdbl_max_po_kernel(
         for w in y + st1 + efk:
             nc.gpsimd.memset(w[:, S:], 0.0)
 
+        half = S // 2
         xs_g = tile("xs_g", [P, S], U8)
-        xw_g = tile("xw_g", [P, S], U32)
+        xw_g = [tile(f"xw_g{h}", [P, half], U32) for h in range(2)]
+        w1d = deal_words("w1", w1w)
         nc.vector.tensor_copy(xs_g[:], xs[:].indirect(offs_t[:]))
-        w1d, w1sd = deal("w1", w1w, w1s)
-        nc.vector.tensor_copy(xw_g[:], xw[:].bitcast(U32).indirect(offs_t[:]))
+        nc.vector.tensor_copy(xw_g[0][:], xw[:].bitcast(U32).indirect(offs_t[:, : half // 16]))
+        w1sd = deal_scales("w1", w1s)
+        nc.vector.tensor_copy(xw_g[1][:], xw[:].bitcast(U32).indirect(offs_t[:, half // 16 :]))
 
         ybank = [ps.tile([P, S], F32, name=f"ybank{t}") for t in range(PACK)]
-        for t in range(PACK):
+        for t, h in [(0, 0), (1, 0), (0, 1), (1, 1), (2, 0), (2, 1), (3, 0), (3, 1)]:
             nc.tensor.matmul_mx(
-                out=ybank[t][:],
+                out=ybank[t][:, h * half : (h + 1) * half],
                 lhsT=w1d[:, 2 * P * t : 2 * P * (t + 1)].bitcast(FP4X4),
                 lhsT_scale=w1sd[:, P * t : P * (t + 1)],
-                rhs=xw_g[:].bitcast(FP8X4),
-                rhs_scale=xs_g[:],
+                rhs=xw_g[h][:].bitcast(FP8X4),
+                rhs_scale=xs_g[:, h * half : (h + 1) * half],
                 start=True,
                 stop=True,
             )
-        w2d, w2sd = deal("w2", w2w, w2s)
+        w2d = deal_words("w2", w2w)
+        w2sd = deal_scales("w2", w2s)
         gain = tile("gain", [P, PACK], F32)
         nc.vector.tensor_scalar(gain[:], unit_t[:], -1.5, None, ALU.mult)
 
@@ -128,10 +139,14 @@ def tile_picked_yrecdbl_max_po_kernel(
             nc.vector.tensor_tensor(out, window[:].indirect(offsets[:]), other[:], ALU.add)
 
         st2 = [tile(f"st2_{t}", [P, S], F32) for t in range(PACK)]
-        low = tile("low", [P, PACK, S], F32)
+        low = tile("low", [P, S // NOUT, PACK, NOUT], F32)
+        planes = tile("planes", [P, S // NOUT, PACK, NOUT], BF16)
 
         def round1(t):
-            nc.scalar.activation(y[t][:, :S], ybank[t][:], ACT.Copy, scale=-1.0 / 1.5)
+            if EV[t] == "S":
+                nc.scalar.activation(y[t][:, :S], ybank[t][:], ACT.Copy, scale=-1.0 / 1.5)
+            else:
+                nc.vector.tensor_scalar(y[t][:, :S], ybank[t][:], -1.0 / 1.5, None, ALU.mult)
             add_partner(f"a1_{t}", G1[t], st1[t][:, :S], y[t], r1_t)
 
         def round2(t):
@@ -140,19 +155,35 @@ def tile_picked_yrecdbl_max_po_kernel(
             nc.scalar.activation(th[:], st2[t][:], ACT.Tanh, scale=-1.5)
             nc.vector.tensor_tensor(efk[t][:, :S], th[:], ef_t[:, t, :], ALU.add)
 
+        b3w = [tile(f"b3w{t}", [P, S], F32) for t in range(PACK)]
+
+        def fetch_b3(t, c0, n):
+            fetch = nc.vector.tensor_copy if G4[t] == "V" else (lambda o, i: nc.scalar.activation(o, i, ACT.Copy))
+            fetch(b3w[t][:, c0 : c0 + n], st1[t][:].indirect(r3_t[:, c0 // 16 : (c0 + n) // 16]))
+
         def round3(t, c0, n):
             cols = slice(c0, c0 + n)
+            qs = slice(c0 // NOUT, (c0 + n) // NOUT)
             sel = r3_t[:, c0 // 16 : (c0 + n) // 16]
-            b3 = tile(f"b3_{t}_{c0}", [P, n], F32)
             st3 = tile(f"st3_{t}_{c0}", [P, n], F32)
-            nc.scalar.activation(b3[:], st1[t][:].indirect(sel), ACT.Copy)
+            if f"D{t}" not in ORDER:
+                fetch_b3(t, c0, n)
             if G3[t] == "V":
                 nc.vector.tensor_tensor(st3[:], efk[t][:].indirect(sel), st2[t][:, cols], ALU.add)
             else:
                 a3 = tile(f"a3_{t}_{c0}", [P, n], F32)
                 nc.scalar.activation(a3[:], efk[t][:].indirect(sel), ACT.Copy)
                 nc.vector.tensor_tensor(st3[:], a3[:], st2[t][:, cols], ALU.add)
-            nc.vector.tensor_tensor(low[:, t, cols], st3[:], b3[:], ALU.min)
+            nc.vector.tensor_tensor(
+                low[:, qs, t, :],
+                st3[:].rearrange("p (q j) -> p q j", j=NOUT),
+                b3w[t][:, cols].rearrange("p (q j) -> p q j", j=NOUT),
+                ALU.min,
+            )
+            if UM[t] == "S":
+                nc.scalar.activation(planes[:, qs, t, :], low[:, qs, t, :], ACT.Copy, scale=gain[:, t : t + 1])
+            else:
+                nc.vector.tensor_scalar(planes[:, qs, t, :], low[:, qs, t, :], gain[:, t : t + 1], None, ALU.mult)
 
         for step in ORDER.split():
             t = int(step[1])
@@ -160,6 +191,8 @@ def tile_picked_yrecdbl_max_po_kernel(
                 round1(t)
             elif step[0] == "B":
                 round2(t)
+            elif step[0] == "D":
+                fetch_b3(t, 0, S)
             else:
                 round3(t, 0, S)
 
@@ -171,44 +204,55 @@ def tile_picked_yrecdbl_max_po_kernel(
             for t in range(PACK):
                 if t not in WHOLE:
                     round3(t, c0, n)
-            hid = tile(f"hid{i}", [P, n * PACK], BF16)
-            nc.vector.tensor_tensor(
-                hid[:].rearrange("p (c i t) -> p c t i", i=2, t=PACK),
-                low[:, :, c0 : c0 + n].rearrange("p t (c i) -> p c t i", i=2),
-                gain[:].unsqueeze(1).unsqueeze(3).to_broadcast([P, n // 2, PACK, 2]),
-                ALU.mult,
-            )
-            h_codes = tile(f"h_codes{i}", [P, n], U32)
-            h_scales = tile(f"h_scales{i}", [P, n], U8)
-            nc.vector.quantize_mx(out=h_codes[:].bitcast(FP8X4), scales=h_scales[:], in_=hid[:])
             for k0 in range(0, n, NOUT):
                 q = (c0 + k0) // NOUT
                 ocols = slice(c0 + k0, c0 + k0 + NOUT)
-                bank = ps.tile([P, PACK, NOUT], F32, name=f"obank{q}")
+                hid = tile(f"hid{q}", [P, NOUT * PACK], BF16)
+                weave = nc.vector.tensor_copy if IL[q] == "V" else nc.scalar.copy
+                weave(
+                    hid[:].rearrange("p (c i t) -> p c t i", i=4, t=PACK),
+                    planes[:, q].rearrange("p t (c i) -> p c t i", i=4),
+                )
+                h_codes = tile(f"h_codes{q}", [P, NOUT], U32)
+                h_scales = tile(f"h_scales{q}", [P, NOUT], U8)
+                nc.vector.quantize_mx(out=h_codes[:].bitcast(FP8X4), scales=h_scales[:], in_=hid[:])
+                if O2[q] == "Y":
+                    halves = [ps.tile([P, 2, NOUT], F32, name=f"obank{q}"), ps.tile([P, 2, NOUT], F32, name="ybank0")]
+                    dst = [halves[t // 2][:, t % 2, :] for t in range(PACK)]
+                else:
+                    bank = ps.tile([P, PACK, NOUT], F32, name=f"obank{q}")
+                    dst = [bank[:, t, :] for t in range(PACK)]
                 for t in range(PACK):
                     nc.tensor.matmul_mx(
-                        out=bank[:, t, :],
+                        out=dst[t],
                         lhsT=w2d[:, 2 * P * t : 2 * P * (t + 1)].bitcast(FP4X4),
                         lhsT_scale=w2sd[:, P * t : P * (t + 1)],
-                        rhs=h_codes[:, k0 : k0 + NOUT].bitcast(FP8X4),
-                        rhs_scale=h_scales[:, k0 : k0 + NOUT],
+                        rhs=h_codes[:].bitcast(FP8X4),
+                        rhs_scale=h_scales[:],
                         start=True,
                         stop=True,
                     )
                 ob = tile(f"ob{q}", [P, NOUT * PACK], BF16)
-                ob_view = ob[:].rearrange("p (c i t) -> p c t i", i=2, t=PACK)
-                bank_view = bank[:].rearrange("p t (c i) -> p c t i", i=2)
-                if O2[q] == "S":
-                    nc.scalar.copy(ob_view, bank_view)
-                else:
-                    nc.vector.tensor_copy(ob_view, bank_view)
                 of = tile(f"of{q}", [P, PACK, NOUT], F32)
-                nc.scalar.copy(of[:], bank[:])
+                ob_view = ob[:].rearrange("p (c i t) -> p c t i", i=2, t=PACK)
+                if O2[q] in "SV":
+                    bank_view = bank[:].rearrange("p t (c i) -> p c t i", i=2)
+                    if O2[q] == "S":
+                        nc.scalar.copy(ob_view, bank_view)
+                    else:
+                        nc.vector.tensor_copy(ob_view, bank_view)
+                    nc.scalar.copy(of[:], bank[:])
+                else:
+                    if O2[q] == "Y":
+                        nc.scalar.copy(of[:, 0:2, :], halves[0][:])
+                        nc.vector.tensor_copy(of[:, 2:4, :], halves[1][:])
+                    else:
+                        nc.scalar.copy(of[:], bank[:])
+                    nc.vector.tensor_copy(ob_view, of[:].rearrange("p t (c i) -> p c t i", i=2))
                 nc.sync.dma_start(out_rows[:, :, ocols], of[:])
                 o_codes = tile(f"o_codes{q}", [P, NOUT], I32)
                 nc.vector.quantize_mx(out=o_codes[:].bitcast(FP8X4), scales=o_scales[:, ocols], in_=ob[:])
                 nc.sync.dma_start(out_words[:, ocols], o_codes[:])
             c0 = c0 + n
         for g in range(4):
-            queue = nc.sync if g % 2 == 0 else nc.scalar
-            queue.dma_start(out_2[0, 4 * g : 4 * g + 4, :].bitcast(I32), o_scales[32 * g : 32 * g + 4, :].bitcast(I32))
+            nc.sync.dma_start(out_2[0, 4 * g : 4 * g + 4, :].bitcast(I32), o_scales[32 * g : 32 * g + 4, :].bitcast(I32))

@@ -18,25 +18,19 @@ ACT = mybir.ActivationFunctionType
 
 P = 128
 PACK = 4
+QUADS = 4
+PER_COL = 16
 SPARE = 16
-NOUT = 128
-G1 = "VVSS"
-G2 = "WWSS"
-G3 = "VVVS"
-O2 = "SSVV"
-PIECES = [128,128,128,128]
-EV = "SSSS"
-UM = "SSSS"
-IL = "VVVV"
-G4 = "SSSS"
-ORDER = "A0 A1 A2 A3 B0 B1 B2 B3 C0 C1 C2 D3"
-WHOLE = [int(s[1]) for s in ORDER.split() if s[0] == "C"]
+HALF = S // 2
+PIECE = 128
+FEEDBACK = 1.5
 
 
 def tile_picked_yrecdbl_max_po_kernel(
     tc, x_words, x_scales, w1_words, w1_scales, ef, unit, w2_words, w2_scales, offs, r1, r2, r3, out_0, out_1, out_2
 ):
     nc = tc.nc
+    last_tile = PACK - 1
     with ExitStack() as ctx:
         sb = ctx.enter_context(tc.tile_pool(name="sb", bufs=1))
         ps = ctx.enter_context(tc.psum_pool(name="ps", bufs=1))
@@ -44,48 +38,63 @@ def tile_picked_yrecdbl_max_po_kernel(
         def tile(name, shape, dtype):
             return sb.tile(shape, dtype, name=name, align_bytes=64)
 
+        def entries(list_tile, c0, n):
+            return list_tile[:, c0 // PER_COL : (c0 + n) // PER_COL]
+
         def load_list(name, src):
-            t = tile(name, [P, S // 16], U16)
-            nc.sync.dma_start(t[:], src)
-            return t
+            list_tile = tile(name, [P, S // PER_COL], U16)
+            nc.sync.dma_start(list_tile[:], src)
+            return list_tile
 
-        def load_scales(name, src, width, queue):
-            t = tile(name, [P, width], U8)
-            for g in range(4):
+        def load_scales(name, src, width):
+            plane = tile(name, [P, width], U8)
+            for g in range(QUADS):
                 rows = src[0, 4 * g : 4 * g + 4, :].bitcast(I32)
-                queue.dma_start(t[32 * g : 32 * g + 32, :].bitcast(I32), rows.unsqueeze(0).to_broadcast([8, 4, width // 4]))
-            return t
+                repeated = rows.unsqueeze(0).to_broadcast([8, 4, width // 4])
+                nc.sync.dma_start(plane[32 * g : 32 * g + 32, :].bitcast(I32), repeated)
+            return plane
 
-        def load_bytes(name, src, queue):
-            t = tile(name, [P, 2 * N], U8)
-            queue.dma_start(t[:].bitcast(I32), src[0].bitcast(I32))
-            return t
+        def load_fp4_words(name, src):
+            words = tile(name, [P, 2 * N], U8)
+            nc.sync.dma_start(words[:].bitcast(I32), src[0].bitcast(I32))
+            return words
 
         def deal_words(name, words):
-            dw = tile(name + "_dw", [P, 2 * N], U8)
+            dealt = tile(name, [P, 2 * N], U8)
             nc.vector.tensor_copy(
-                out=dw[:].rearrange("p (t m b) -> p t m b", t=PACK, b=2),
+                out=dealt[:].rearrange("p (t m b) -> p t m b", t=PACK, b=2),
                 in_=words[:].rearrange("p (m t b) -> p t m b", t=PACK, b=2),
             )
-            return dw
+            return dealt
 
-        def deal_scales(name, scales):
-            ds = tile(name + "_ds", [P, N], U8)
+        def deal_scales(name, plane):
+            dealt = tile(name, [P, N], U8)
             nc.vector.tensor_copy(
-                out=ds[:].rearrange("p (t m) -> p t m", t=PACK),
-                in_=scales[:].rearrange("p (m t) -> p t m", t=PACK),
+                out=dealt[:].rearrange("p (t m) -> p t m", t=PACK),
+                in_=plane[:].rearrange("p (m t) -> p t m", t=PACK),
             )
-            return ds
+            return dealt
+
+        def product(out, w_words, w_plane, t, codes, scales):
+            nc.tensor.matmul_mx(
+                out=out,
+                lhsT=w_words[:, 2 * P * t : 2 * P * (t + 1)].bitcast(FP4X4),
+                lhsT_scale=w_plane[:, P * t : P * (t + 1)],
+                rhs=codes.bitcast(FP8X4),
+                rhs_scale=scales,
+                start=True,
+                stop=True,
+            )
 
         offs_t = load_list("offs_t", offs)
-        w1w = load_bytes("w1w", w1_words, nc.sync)
-        xs = load_scales("xs", x_scales, T, nc.sync)
-        xw = tile("xw", [P, T], I32)
-        nc.sync.dma_start(xw[:], x_words[0].rearrange("p n t -> p (n t)").bitcast(I32))
-        w1s = load_scales("w1s", w1_scales, N, nc.sync)
+        w1_raw = load_fp4_words("w1_raw", w1_words)
+        x_plane = load_scales("x_plane", x_scales, T)
+        x_table = tile("x_table", [P, T], I32)
+        nc.sync.dma_start(x_table[:], x_words[0].rearrange("p n t -> p (n t)").bitcast(I32))
+        w1_raw_plane = load_scales("w1_raw_plane", w1_scales, N)
         r1_t = load_list("r1_t", r1)
-        w2w = load_bytes("w2w", w2_words, nc.sync)
-        w2s = load_scales("w2s", w2_scales, N, nc.sync)
+        w2_raw = load_fp4_words("w2_raw", w2_words)
+        w2_raw_plane = load_scales("w2_raw_plane", w2_scales, N)
         r2_t = load_list("r2_t", r2)
         r3_t = load_list("r3_t", r3)
         unit_t = tile("unit_t", [P, PACK], F32)
@@ -95,164 +104,124 @@ def tile_picked_yrecdbl_max_po_kernel(
 
         y = [tile(f"y{t}", [P, S + SPARE], F32) for t in range(PACK)]
         st1 = [tile(f"st1_{t}", [P, S + SPARE], F32) for t in range(PACK)]
-        efk = [tile(f"efk{t}", [P, S + SPARE], F32) for t in range(PACK)]
-        for w in y + st1 + efk:
-            nc.gpsimd.memset(w[:, S:], 0.0)
+        efk = [tile(f"efk{t}", [P, S + SPARE], F32) for t in range(last_tile)] + [tile("efk_last", [P, S], F32)]
+        for window in y + st1 + efk[:last_tile]:
+            nc.gpsimd.memset(window[:, S:], 0.0)
 
-        half = S // 2
-        xs_g = tile("xs_g", [P, S], U8)
-        xw_g = [tile(f"xw_g{h}", [P, half], U32) for h in range(2)]
-        w1d = deal_words("w1", w1w)
-        nc.vector.tensor_copy(xs_g[:], xs[:].indirect(offs_t[:]))
-        nc.vector.tensor_copy(xw_g[0][:], xw[:].bitcast(U32).indirect(offs_t[:, : half // 16]))
-        w1sd = deal_scales("w1", w1s)
-        nc.vector.tensor_copy(xw_g[1][:], xw[:].bitcast(U32).indirect(offs_t[:, half // 16 :]))
+        x_scales_picked = tile("x_scales_picked", [P, S], U8)
+        x_picked = [tile(f"x_picked{h}", [P, HALF], U32) for h in range(2)]
+        w1 = deal_words("w1", w1_raw)
+        nc.vector.tensor_copy(x_scales_picked[:], x_plane[:].indirect(offs_t[:]))
+        nc.vector.tensor_copy(x_picked[0][:], x_table[:].bitcast(U32).indirect(entries(offs_t, 0, HALF)))
+        w1_plane = deal_scales("w1_plane", w1_raw_plane)
+        nc.vector.tensor_copy(x_picked[1][:], x_table[:].bitcast(U32).indirect(entries(offs_t, HALF, HALF)))
 
-        ybank = [ps.tile([P, S], F32, name=f"ybank{t}") for t in range(PACK)]
-        for t, h in [(0, 0), (1, 0), (0, 1), (1, 1), (2, 0), (2, 1), (3, 0), (3, 1)]:
-            nc.tensor.matmul_mx(
-                out=ybank[t][:, h * half : (h + 1) * half],
-                lhsT=w1d[:, 2 * P * t : 2 * P * (t + 1)].bitcast(FP4X4),
-                lhsT_scale=w1sd[:, P * t : P * (t + 1)],
-                rhs=xw_g[h][:].bitcast(FP8X4),
-                rhs_scale=xs_g[:, h * half : (h + 1) * half],
-                start=True,
-                stop=True,
-            )
-        w2d = deal_words("w2", w2w)
-        w2sd = deal_scales("w2", w2s)
+        y_bank = [ps.tile([P, S], F32, name=f"y_bank{t}") for t in range(PACK)]
+        y0_right = ps.tile([P, HALF], F32, name="out_bank2")
+        for t in range(PACK):
+            for h in range(2):
+                cols = slice(h * HALF, (h + 1) * HALF)
+                dst = y0_right[:] if (t, h) == (0, 1) else y_bank[t][:, cols]
+                product(dst, w1, w1_plane, t, x_picked[h][:], x_scales_picked[:, cols])
+        w2 = deal_words("w2", w2_raw)
+        w2_plane = deal_scales("w2_plane", w2_raw_plane)
         gain = tile("gain", [P, PACK], F32)
-        nc.vector.tensor_scalar(gain[:], unit_t[:], -1.5, None, ALU.mult)
+        nc.vector.tensor_scalar(gain[:], unit_t[:], -FEEDBACK, None, ALU.mult)
 
-        def add_partner(name, how, out, window, offsets):
+        def add_partner(name, t, out, window, list_tile, duplicate):
             other = tile(name, [P, S], F32)
-            if how == "S":
-                nc.scalar.activation(other[:], window[:].indirect(offsets[:]), ACT.Copy)
+            if t % 2 == 1:
+                nc.scalar.activation(other[:], window[:].indirect(list_tile[:]), ACT.Copy)
                 nc.vector.tensor_tensor(out, other[:], window[:, :S], ALU.add)
-                return
-            if how == "V":
-                nc.vector.tensor_copy(other[:], window[:, :S])
-            elif how == "W":
-                nc.scalar.copy(other[:], window[:, :S])
             else:
-                nc.sync.dma_start(other[:], window[:, :S])
-            nc.vector.tensor_tensor(out, window[:].indirect(offsets[:]), other[:], ALU.add)
+                duplicate(other[:], window[:, :S])
+                nc.vector.tensor_tensor(out, window[:].indirect(list_tile[:]), other[:], ALU.add)
 
         st2 = [tile(f"st2_{t}", [P, S], F32) for t in range(PACK)]
-        low = tile("low", [P, S // NOUT, PACK, NOUT], F32)
-        planes = tile("planes", [P, S // NOUT, PACK, NOUT], BF16)
+        low = tile("low", [P, S // PIECE, PACK, PIECE], F32)
 
-        def round1(t):
-            if EV[t] == "S":
-                nc.scalar.activation(y[t][:, :S], ybank[t][:], ACT.Copy, scale=-1.0 / 1.5)
+        for t in range(PACK):
+            if t == 0:
+                nc.scalar.activation(y[t][:, :HALF], y_bank[t][:, :HALF], ACT.Copy, scale=-1.0 / FEEDBACK)
+                nc.vector.tensor_scalar(y[t][:, HALF:S], y0_right[:], -1.0 / FEEDBACK, None, ALU.mult)
             else:
-                nc.vector.tensor_scalar(y[t][:, :S], ybank[t][:], -1.0 / 1.5, None, ALU.mult)
-            add_partner(f"a1_{t}", G1[t], st1[t][:, :S], y[t], r1_t)
+                nc.scalar.activation(y[t][:, :S], y_bank[t][:], ACT.Copy, scale=-1.0 / FEEDBACK)
+            add_partner(f"a1_{t}", t, st1[t][:, :S], y[t], r1_t, nc.vector.tensor_copy)
 
-        def round2(t):
-            add_partner(f"a2_{t}", G2[t], st2[t][:], st1[t], r2_t)
-            th = tile(f"th{t}", [P, S], F32)
-            nc.scalar.activation(th[:], st2[t][:], ACT.Tanh, scale=-1.5)
-            nc.vector.tensor_tensor(efk[t][:, :S], th[:], ef_t[:, t, :], ALU.add)
+        for t in range(PACK):
+            add_partner(f"a2_{t}", t, st2[t][:], st1[t], r2_t, nc.scalar.copy)
+            bounded = tile(f"work{t}", [P, S], F32)
+            nc.scalar.activation(bounded[:], st2[t][:], ACT.Tanh, scale=-FEEDBACK)
+            nc.vector.tensor_tensor(efk[t][:, :S], bounded[:], ef_t[:, t, :], ALU.add)
 
-        b3w = [tile(f"b3w{t}", [P, S], F32) for t in range(PACK)]
+        b3 = [tile(f"work{t}", [P, S], F32) for t in range(PACK)]
 
-        def fetch_b3(t, c0, n):
-            fetch = nc.vector.tensor_copy if G4[t] == "V" else (lambda o, i: nc.scalar.activation(o, i, ACT.Copy))
-            fetch(b3w[t][:, c0 : c0 + n], st1[t][:].indirect(r3_t[:, c0 // 16 : (c0 + n) // 16]))
-
-        def round3(t, c0, n):
+        def round_three(t, c0, n):
             cols = slice(c0, c0 + n)
-            qs = slice(c0 // NOUT, (c0 + n) // NOUT)
-            sel = r3_t[:, c0 // 16 : (c0 + n) // 16]
+            offsets = entries(r3_t, c0, n)
             st3 = tile(f"st3_{t}_{c0}", [P, n], F32)
-            if f"D{t}" not in ORDER:
-                fetch_b3(t, c0, n)
-            if G3[t] == "V":
-                nc.vector.tensor_tensor(st3[:], efk[t][:].indirect(sel), st2[t][:, cols], ALU.add)
-            else:
-                a3 = tile(f"a3_{t}_{c0}", [P, n], F32)
-                nc.scalar.activation(a3[:], efk[t][:].indirect(sel), ACT.Copy)
+            nc.scalar.activation(b3[t][:, cols], st1[t][:].indirect(offsets), ACT.Copy)
+            if t == last_tile:
+                a3 = tile(f"a3_{c0}", [P, n], F32)
+                nc.scalar.activation(a3[:], efk[t][:].indirect(offsets), ACT.Copy)
                 nc.vector.tensor_tensor(st3[:], a3[:], st2[t][:, cols], ALU.add)
+            else:
+                nc.vector.tensor_tensor(st3[:], efk[t][:].indirect(offsets), st2[t][:, cols], ALU.add)
             nc.vector.tensor_tensor(
-                low[:, qs, t, :],
-                st3[:].rearrange("p (q j) -> p q j", j=NOUT),
-                b3w[t][:, cols].rearrange("p (q j) -> p q j", j=NOUT),
+                low[:, c0 // PIECE : (c0 + n) // PIECE, t, :],
+                st3[:].rearrange("p (q j) -> p q j", j=PIECE),
+                b3[t][:, cols].rearrange("p (q j) -> p q j", j=PIECE),
                 ALU.min,
             )
-            if UM[t] == "S":
-                nc.scalar.activation(planes[:, qs, t, :], low[:, qs, t, :], ACT.Copy, scale=gain[:, t : t + 1])
-            else:
-                nc.vector.tensor_scalar(planes[:, qs, t, :], low[:, qs, t, :], gain[:, t : t + 1], None, ALU.mult)
-
-        for step in ORDER.split():
-            t = int(step[1])
-            if step[0] == "A":
-                round1(t)
-            elif step[0] == "B":
-                round2(t)
-            elif step[0] == "D":
-                fetch_b3(t, 0, S)
-            else:
-                round3(t, 0, S)
 
         out_rows = out_0.rearrange("(p t) j -> p t j", t=PACK)
         out_words = out_1[0].rearrange("p n t -> p (n t)").bitcast(I32)
-        o_scales = tile("o_scales", [P, S], U8)
-        c0 = 0
-        for i, n in enumerate(PIECES):
-            for t in range(PACK):
-                if t not in WHOLE:
-                    round3(t, c0, n)
-            for k0 in range(0, n, NOUT):
-                q = (c0 + k0) // NOUT
-                ocols = slice(c0 + k0, c0 + k0 + NOUT)
-                hid = tile(f"hid{q}", [P, NOUT * PACK], BF16)
-                weave = nc.vector.tensor_copy if IL[q] == "V" else nc.scalar.copy
-                weave(
-                    hid[:].rearrange("p (c i t) -> p c t i", i=4, t=PACK),
-                    planes[:, q].rearrange("p t (c i) -> p c t i", i=4),
-                )
-                h_codes = tile(f"h_codes{q}", [P, NOUT], U32)
-                h_scales = tile(f"h_scales{q}", [P, NOUT], U8)
-                nc.vector.quantize_mx(out=h_codes[:].bitcast(FP8X4), scales=h_scales[:], in_=hid[:])
-                if O2[q] == "Y":
-                    halves = [ps.tile([P, 2, NOUT], F32, name=f"obank{q}"), ps.tile([P, 2, NOUT], F32, name="ybank0")]
-                    dst = [halves[t // 2][:, t % 2, :] for t in range(PACK)]
-                else:
-                    bank = ps.tile([P, PACK, NOUT], F32, name=f"obank{q}")
-                    dst = [bank[:, t, :] for t in range(PACK)]
+        out_plane = tile("out_plane", [P, S], U8)
+
+        def woven(bf16_tile):
+            return bf16_tile[:].rearrange("p (c i t) -> p c t i", i=2, t=PACK)
+
+        def by_pairs(rows):
+            return rows.rearrange("p t (c i) -> p c t i", i=2)
+
+        def finish_piece(q):
+            cols = slice(q * PIECE, (q + 1) * PIECE)
+            hid = tile(f"hid{q}", [P, PIECE * PACK], BF16)
+            gains = gain[:].unsqueeze(1).unsqueeze(3).to_broadcast([P, PIECE // 2, PACK, 2])
+            nc.vector.tensor_tensor(woven(hid), by_pairs(low[:, q]), gains, ALU.mult)
+            hid_codes = tile(f"hid_codes{q}", [P, PIECE], U32)
+            hid_scales = tile(f"hid_scales{q}", [P, PIECE], U8)
+            nc.vector.quantize_mx(out=hid_codes[:].bitcast(FP8X4), scales=hid_scales[:], in_=hid[:])
+
+            result = tile(f"result{q}", [P, PACK, PIECE], F32)
+            if q < S // PIECE - 1:
+                bank = ps.tile([P, PACK, PIECE], F32, name=f"out_bank{q}")
                 for t in range(PACK):
-                    nc.tensor.matmul_mx(
-                        out=dst[t],
-                        lhsT=w2d[:, 2 * P * t : 2 * P * (t + 1)].bitcast(FP4X4),
-                        lhsT_scale=w2sd[:, P * t : P * (t + 1)],
-                        rhs=h_codes[:].bitcast(FP8X4),
-                        rhs_scale=h_scales[:],
-                        start=True,
-                        stop=True,
-                    )
-                ob = tile(f"ob{q}", [P, NOUT * PACK], BF16)
-                of = tile(f"of{q}", [P, PACK, NOUT], F32)
-                ob_view = ob[:].rearrange("p (c i t) -> p c t i", i=2, t=PACK)
-                if O2[q] in "SV":
-                    bank_view = bank[:].rearrange("p t (c i) -> p c t i", i=2)
-                    if O2[q] == "S":
-                        nc.scalar.copy(ob_view, bank_view)
-                    else:
-                        nc.vector.tensor_copy(ob_view, bank_view)
-                    nc.scalar.copy(of[:], bank[:])
-                else:
-                    if O2[q] == "Y":
-                        nc.scalar.copy(of[:, 0:2, :], halves[0][:])
-                        nc.vector.tensor_copy(of[:, 2:4, :], halves[1][:])
-                    else:
-                        nc.scalar.copy(of[:], bank[:])
-                    nc.vector.tensor_copy(ob_view, of[:].rearrange("p t (c i) -> p c t i", i=2))
-                nc.sync.dma_start(out_rows[:, :, ocols], of[:])
-                o_codes = tile(f"o_codes{q}", [P, NOUT], I32)
-                nc.vector.quantize_mx(out=o_codes[:].bitcast(FP8X4), scales=o_scales[:, ocols], in_=ob[:])
-                nc.sync.dma_start(out_words[:, ocols], o_codes[:])
-            c0 = c0 + n
-        for g in range(4):
-            nc.sync.dma_start(out_2[0, 4 * g : 4 * g + 4, :].bitcast(I32), o_scales[32 * g : 32 * g + 4, :].bitcast(I32))
+                    product(bank[:, t, :], w2, w2_plane, t, hid_codes[:], hid_scales[:])
+                nc.scalar.copy(result[:], bank[:])
+            else:
+                pair = [ps.tile([P, 2, PIECE], F32, name=name) for name in (f"out_bank{q}", "y_bank0")]
+                for t in range(PACK):
+                    product(pair[t // 2][:, t % 2, :], w2, w2_plane, t, hid_codes[:], hid_scales[:])
+                nc.scalar.copy(result[:, :2, :], pair[0][:])
+                nc.vector.tensor_copy(result[:, 2:, :], pair[1][:])
+
+            rounded = tile(f"rounded{q}", [P, PIECE * PACK], BF16)
+            nc.vector.tensor_copy(woven(rounded), by_pairs(result[:]))
+            nc.sync.dma_start(out_rows[:, :, cols], result[:])
+            out_codes = tile(f"out_codes{q}", [P, PIECE], I32)
+            nc.vector.quantize_mx(out=out_codes[:].bitcast(FP8X4), scales=out_plane[:, cols], in_=rounded[:])
+            nc.sync.dma_start(out_words[:, cols], out_codes[:])
+
+        for t in range(last_tile):
+            round_three(t, 0, S)
+        for c0 in range(0, S, HALF):
+            round_three(last_tile, c0, HALF)
+            for q in range(c0 // PIECE, (c0 + HALF) // PIECE):
+                finish_piece(q)
+
+        for g in range(QUADS):
+            queue = nc.sync if g % 2 == 0 else nc.scalar
+            queue.dma_start(
+                out_2[0, 4 * g : 4 * g + 4, :].bitcast(I32), out_plane[32 * g : 32 * g + 4, :].bitcast(I32)
+            )

@@ -194,20 +194,21 @@ def tile_picked_yrecdbl_max_po_kernel(
             nc.vector.quantize_mx(out=hid_codes[:].bitcast(FP8X4), scales=hid_scales[:], in_=hid[:])
 
             result = tile(f"result{q}", [P, PACK, PIECE], F32)
+            rounded = tile(f"rounded{q}", [P, PIECE * PACK], BF16)
             if q < S // PIECE - 1:
                 bank = ps.tile([P, PACK, PIECE], F32, name=f"out_bank{q}")
                 for t in range(PACK):
                     product(bank[:, t, :], w2, w2_plane, t, hid_codes[:], hid_scales[:])
                 nc.scalar.copy(result[:], bank[:])
+                nc.scalar.copy(woven(rounded), by_pairs(bank[:]))
             else:
                 pair = [ps.tile([P, 2, PIECE], F32, name=name) for name in (f"out_bank{q}", "y_bank0")]
                 for t in range(PACK):
                     product(pair[t // 2][:, t % 2, :], w2, w2_plane, t, hid_codes[:], hid_scales[:])
                 nc.scalar.copy(result[:, :2, :], pair[0][:])
                 nc.vector.tensor_copy(result[:, 2:, :], pair[1][:])
+                nc.vector.tensor_copy(woven(rounded), by_pairs(result[:]))
 
-            rounded = tile(f"rounded{q}", [P, PIECE * PACK], BF16)
-            nc.vector.tensor_copy(woven(rounded), by_pairs(result[:]))
             nc.sync.dma_start(out_rows[:, :, cols], result[:])
             out_codes = tile(f"out_codes{q}", [P, PIECE], I32)
             nc.vector.quantize_mx(out=out_codes[:].bitcast(FP8X4), scales=out_plane[:, cols], in_=rounded[:])

@@ -23,6 +23,7 @@ PER_COL = 16
 SPARE = 16
 HALF = S // 2
 PIECE = 128
+SCALAR_ROUNDS = 2
 FEEDBACK = 1.5
 
 
@@ -200,13 +201,15 @@ def tile_picked_yrecdbl_max_po_kernel(
                 for t in range(PACK):
                     product(bank[:, t, :], w2, w2_plane, t, hid_codes[:], hid_scales[:])
                 nc.scalar.copy(result[:], bank[:])
-                nc.scalar.copy(woven(rounded), by_pairs(bank[:]))
+                if q < SCALAR_ROUNDS:
+                    nc.scalar.copy(woven(rounded), by_pairs(bank[:]))
             else:
                 pair = [ps.tile([P, 2, PIECE], F32, name=name) for name in (f"out_bank{q}", "y_bank0")]
                 for t in range(PACK):
                     product(pair[t // 2][:, t % 2, :], w2, w2_plane, t, hid_codes[:], hid_scales[:])
                 nc.scalar.copy(result[:, :2, :], pair[0][:])
                 nc.vector.tensor_copy(result[:, 2:, :], pair[1][:])
+            if q >= SCALAR_ROUNDS:
                 nc.vector.tensor_copy(woven(rounded), by_pairs(result[:]))
 
             nc.sync.dma_start(out_rows[:, :, cols], result[:])

from contextlib import ExitStack

import concourse.mybir as mybir

K, T, S, N, H = 512, 1024, 512, 512, 512
FLOPS = 2 * K * H * S + 2 * H * N * S

F32 = mybir.dt.float32
BF16 = mybir.dt.bfloat16
I32 = mybir.dt.int32
U32 = mybir.dt.uint32
U16 = mybir.dt.uint16
U8 = mybir.dt.uint8
FP8X4 = mybir.dt.float8_e4m3fn_x4
FP4X4 = mybir.dt.float4_e2m1fn_x4
ALU = mybir.AluOpType
ACT = mybir.ActivationFunctionType

P = 128
PACK = 4
QUADS = 4
PER_COL = 16
SPARE = 16
HALF = S // 2
PIECE = 128
SCALAR_ROUNDS = 2
FEEDBACK = 1.5


def tile_picked_yrecdbl_max_po_kernel(
    tc, x_words, x_scales, w1_words, w1_scales, ef, unit, w2_words, w2_scales, offs, r1, r2, r3, out_0, out_1, out_2
):
    nc = tc.nc
    last_tile = PACK - 1
    with ExitStack() as ctx:
        sb = ctx.enter_context(tc.tile_pool(name="sb", bufs=1))
        ps = ctx.enter_context(tc.psum_pool(name="ps", bufs=1))

        def tile(name, shape, dtype):
            return sb.tile(shape, dtype, name=name, align_bytes=64)

        def entries(list_tile, c0, n):
            return list_tile[:, c0 // PER_COL : (c0 + n) // PER_COL]

        def load_list(name, src):
            list_tile = tile(name, [P, S // PER_COL], U16)
            nc.sync.dma_start(list_tile[:], src)
            return list_tile

        def load_scales(name, src, width):
            plane = tile(name, [P, width], U8)
            for g in range(QUADS):
                rows = src[0, 4 * g : 4 * g + 4, :].bitcast(I32)
                repeated = rows.unsqueeze(0).to_broadcast([8, 4, width // 4])
                nc.sync.dma_start(plane[32 * g : 32 * g + 32, :].bitcast(I32), repeated)
            return plane

        def load_fp4_words(name, src):
            words = tile(name, [P, 2 * N], U8)
            nc.sync.dma_start(words[:].bitcast(I32), src[0].bitcast(I32))
            return words

        def deal_words(name, words):
            dealt = tile(name, [P, 2 * N], U8)
            nc.vector.tensor_copy(
                out=dealt[:].rearrange("p (t m b) -> p t m b", t=PACK, b=2),
                in_=words[:].rearrange("p (m t b) -> p t m b", t=PACK, b=2),
            )
            return dealt

        def deal_scales(name, plane):
            dealt = tile(name, [P, N], U8)
            nc.vector.tensor_copy(
                out=dealt[:].rearrange("p (t m) -> p t m", t=PACK),
                in_=plane[:].rearrange("p (m t) -> p t m", t=PACK),
            )
            return dealt

        def product(out, w_words, w_plane, t, codes, scales):
            nc.tensor.matmul_mx(
                out=out,
                lhsT=w_words[:, 2 * P * t : 2 * P * (t + 1)].bitcast(FP4X4),
                lhsT_scale=w_plane[:, P * t : P * (t + 1)],
                rhs=codes.bitcast(FP8X4),
                rhs_scale=scales,
                start=True,
                stop=True,
            )

        offs_t = load_list("offs_t", offs)
        w1_raw = load_fp4_words("w1_raw", w1_words)
        x_plane = load_scales("x_plane", x_scales, T)
        x_table = tile("x_table", [P, T], I32)
        nc.sync.dma_start(x_table[:], x_words[0].rearrange("p n t -> p (n t)").bitcast(I32))
        w1_raw_plane = load_scales("w1_raw_plane", w1_scales, N)
        r1_t = load_list("r1_t", r1)
        w2_raw = load_fp4_words("w2_raw", w2_words)
        w2_raw_plane = load_scales("w2_raw_plane", w2_scales, N)
        r2_t = load_list("r2_t", r2)
        r3_t = load_list("r3_t", r3)
        unit_t = tile("unit_t", [P, PACK], F32)
        nc.sync.dma_start(unit_t[:], unit.rearrange("(p t) o -> p (t o)", t=PACK))
        ef_t = tile("ef_t", [P, PACK, S], F32)
        nc.sync.dma_start(ef_t[:], ef.rearrange("(p t) j -> p t j", t=PACK))

        y = [tile(f"y{t}", [P, S + SPARE], F32) for t in range(PACK)]
        st1 = [tile(f"st1_{t}", [P, S + SPARE], F32) for t in range(PACK)]
        efk = [tile(f"efk{t}", [P, S + SPARE], F32) for t in range(last_tile)] + [tile("efk_last", [P, S], F32)]
        for window in y + st1 + efk[:last_tile]:
            nc.gpsimd.memset(window[:, S:], 0.0)

        x_scales_picked = tile("x_scales_picked", [P, S], U8)
        x_picked = [tile(f"x_picked{h}", [P, HALF], U32) for h in range(2)]
        w1 = deal_words("w1", w1_raw)
        nc.vector.tensor_copy(x_scales_picked[:], x_plane[:].indirect(offs_t[:]))
        nc.vector.tensor_copy(x_picked[0][:], x_table[:].bitcast(U32).indirect(entries(offs_t, 0, HALF)))
        w1_plane = deal_scales("w1_plane", w1_raw_plane)
        nc.vector.tensor_copy(x_picked[1][:], x_table[:].bitcast(U32).indirect(entries(offs_t, HALF, HALF)))

        y_bank = [ps.tile([P, S], F32, name=f"y_bank{t}") for t in range(PACK)]
        y0_right = ps.tile([P, HALF], F32, name="out_bank2")
        for t in range(PACK):
            for h in range(2):
                cols = slice(h * HALF, (h + 1) * HALF)
                dst = y0_right[:] if (t, h) == (0, 1) else y_bank[t][:, cols]
                product(dst, w1, w1_plane, t, x_picked[h][:], x_scales_picked[:, cols])
        w2 = deal_words("w2", w2_raw)
        w2_plane = deal_scales("w2_plane", w2_raw_plane)
        gain = tile("gain", [P, PACK], F32)
        nc.vector.tensor_scalar(gain[:], unit_t[:], -FEEDBACK, None, ALU.mult)

        def add_partner(name, t, out, window, list_tile, duplicate):
            other = tile(name, [P, S], F32)
            if t % 2 == 1:
                nc.scalar.activation(other[:], window[:].indirect(list_tile[:]), ACT.Copy)
                nc.vector.tensor_tensor(out, other[:], window[:, :S], ALU.add)
            else:
                duplicate(other[:], window[:, :S])
                nc.vector.tensor_tensor(out, window[:].indirect(list_tile[:]), other[:], ALU.add)

        st2 = [tile(f"st2_{t}", [P, S], F32) for t in range(PACK)]
        low = tile("low", [P, S // PIECE, PACK, PIECE], F32)

        for t in range(PACK):
            if t == 0:
                nc.scalar.activation(y[t][:, :HALF], y_bank[t][:, :HALF], ACT.Copy, scale=-1.0 / FEEDBACK)
                nc.vector.tensor_scalar(y[t][:, HALF:S], y0_right[:], -1.0 / FEEDBACK, None, ALU.mult)
            else:
                nc.scalar.activation(y[t][:, :S], y_bank[t][:], ACT.Copy, scale=-1.0 / FEEDBACK)
            add_partner(f"a1_{t}", t, st1[t][:, :S], y[t], r1_t, nc.vector.tensor_copy)

        for t in range(PACK):
            add_partner(f"a2_{t}", t, st2[t][:], st1[t], r2_t, nc.scalar.copy)
            bounded = tile(f"work{t}", [P, S], F32)
            nc.scalar.activation(bounded[:], st2[t][:], ACT.Tanh, scale=-FEEDBACK)
            nc.vector.tensor_tensor(efk[t][:, :S], bounded[:], ef_t[:, t, :], ALU.add)

        b3 = [tile(f"work{t}", [P, S], F32) for t in range(PACK)]

        def round_three(t, c0, n):
            cols = slice(c0, c0 + n)
            offsets = entries(r3_t, c0, n)
            st3 = tile(f"st3_{t}_{c0}", [P, n], F32)
            nc.scalar.activation(b3[t][:, cols], st1[t][:].indirect(offsets), ACT.Copy)
            if t == last_tile:
                a3 = tile(f"a3_{c0}", [P, n], F32)
                nc.scalar.activation(a3[:], efk[t][:].indirect(offsets), ACT.Copy)
                nc.vector.tensor_tensor(st3[:], a3[:], st2[t][:, cols], ALU.add)
            else:
                nc.vector.tensor_tensor(st3[:], efk[t][:].indirect(offsets), st2[t][:, cols], ALU.add)
            nc.vector.tensor_tensor(
                low[:, c0 // PIECE : (c0 + n) // PIECE, t, :],
                st3[:].rearrange("p (q j) -> p q j", j=PIECE),
                b3[t][:, cols].rearrange("p (q j) -> p q j", j=PIECE),
                ALU.min,
            )

        out_rows = out_0.rearrange("(p t) j -> p t j", t=PACK)
        out_words = out_1[0].rearrange("p n t -> p (n t)").bitcast(I32)
        out_plane = tile("out_plane", [P, S], U8)

        def woven(bf16_tile):
            return bf16_tile[:].rearrange("p (c i t) -> p c t i", i=2, t=PACK)

        def by_pairs(rows):
            return rows.rearrange("p t (c i) -> p c t i", i=2)

        def finish_piece(q):
            cols = slice(q * PIECE, (q + 1) * PIECE)
            hid = tile(f"hid{q}", [P, PIECE * PACK], BF16)
            gains = gain[:].unsqueeze(1).unsqueeze(3).to_broadcast([P, PIECE // 2, PACK, 2])
            nc.vector.tensor_tensor(woven(hid), by_pairs(low[:, q]), gains, ALU.mult)
            hid_codes = tile(f"hid_codes{q}", [P, PIECE], U32)
            hid_scales = tile(f"hid_scales{q}", [P, PIECE], U8)
            nc.vector.quantize_mx(out=hid_codes[:].bitcast(FP8X4), scales=hid_scales[:], in_=hid[:])

            result = tile(f"result{q}", [P, PACK, PIECE], F32)
            rounded = tile(f"rounded{q}", [P, PIECE * PACK], BF16)
            if q < S // PIECE - 1:
                bank = ps.tile([P, PACK, PIECE], F32, name=f"out_bank{q}")
                for t in range(PACK):
                    product(bank[:, t, :], w2, w2_plane, t, hid_codes[:], hid_scales[:])
                nc.scalar.copy(result[:], bank[:])
                if q < SCALAR_ROUNDS:
                    nc.scalar.copy(woven(rounded), by_pairs(bank[:]))
            else:
                pair = [ps.tile([P, 2, PIECE], F32, name=name) for name in (f"out_bank{q}", "y_bank0")]
                for t in range(PACK):
                    product(pair[t // 2][:, t % 2, :], w2, w2_plane, t, hid_codes[:], hid_scales[:])
                nc.scalar.copy(result[:, :2, :], pair[0][:])
                nc.vector.tensor_copy(result[:, 2:, :], pair[1][:])
            if q >= SCALAR_ROUNDS:
                nc.vector.tensor_copy(woven(rounded), by_pairs(result[:]))

            nc.sync.dma_start(out_rows[:, :, cols], result[:])
            out_codes = tile(f"out_codes{q}", [P, PIECE], I32)
            nc.vector.quantize_mx(out=out_codes[:].bitcast(FP8X4), scales=out_plane[:, cols], in_=rounded[:])
            nc.sync.dma_start(out_words[:, cols], out_codes[:])

        for t in range(last_tile):
            round_three(t, 0, S)
        for c0 in range(0, S, HALF):
            round_three(last_tile, c0, HALF)
            for q in range(c0 // PIECE, (c0 + HALF) // PIECE):
                finish_piece(q)

        for g in range(QUADS):
            queue = nc.sync if g % 2 == 0 else nc.scalar
            queue.dma_start(
                out_2[0, 4 * g : 4 * g + 4, :].bitcast(I32), out_plane[32 * g : 32 * g + 4, :].bitcast(I32)
            )
